import numpy as np, ml_dtypes
CORES = [144,200,272,328,400,456]
N = 6
import mx_ref
NC, G, MB = 128, 2, 1
C = np.float32(0.041)
BF = ml_dtypes.bfloat16
def cut(t, i, w=512):
    return t[:, w * i:w * i + w]
def tile(rs):
    return np.stack(rs, axis=2).reshape(128, -1).astype(BF)
def layer(w, X):
    out = []
    for i in range(G):
        for t in range(len(X)):
            p = mx_ref.matmul(mx_ref.quantize(cut(w, len(X) * i + t)), X[t])
            z = p if t == 0 else z + p
        out.append(z)
    return out
def act(Z):
    return [np.maximum(s * z, 0) * C for z in Z for s in (1, -1)]
def masked(U, Z):
    return [(s * u * (s * z > 0)) * C for u, z in zip(U, Z) for s in (1, -1)]
def setup_inputs(rng):
    def f(*shape):
        return mx_ref.flush((rng.standard_normal(shape, dtype=np.float32) * np.exp2(rng.integers(-2, 3, shape[:-1] + (1,)))).astype(BF))
    return {"x": f(N, 128, MB * 4 * NC), "e": f(N, 128, MB * 4 * NC), "w": f(N, 128, G * 512), "v": f(N, 128, G * 512)}
def setup_inputs_blocks(rng):
    d = setup_inputs(rng)
    for k in ("x", "e"): d[k] = mx_ref.spread(d[k], rng, 4)
    for k in ("w", "v"): d[k] = mx_ref.spread(d[k], rng, 1)
    return d
def setup_inputs_wide(rng):
    d = setup_inputs(rng)
    for k in ("x", "e"): d[k] = mx_ref.flush((d[k].astype(np.float32) * np.exp2(rng.integers(-8, 9, (N, 1, 1))).astype(np.float32)).astype(BF))
    return d
def setup_inputs_zeros(rng):
    d = setup_inputs(rng); v = d["x"].reshape(N, 128, -1, 4).copy()
    v[np.broadcast_to((rng.random((N, 1, v.shape[2], 1)) < 0.33), v.shape)] = 0
    d["x"] = v.reshape(d["x"].shape)
    return d
def reference(x, e, w, v):
    y = np.full((N, 128, MB * G * NC), np.nan, np.float32)
    for m in range(MB):
        a = mx_ref.quantize(cut(x[N - 1], m, 4 * NC)); Z = []
        for s in range(N):
            Z.append(layer(w[s], [a]))
            if s < N - 1: a = mx_ref.quantize(tile(act(Z[s])))
        b = mx_ref.quantize(cut(e[0], m, 4 * NC))
        for s in range(N - 1, 0, -1):
            b = mx_ref.quantize(tile(masked(layer(v[s], [b]), Z[s])))
        U = layer(v[0], [b])
        for i in range(G):
            y[0][:, NC * (G * m + i):NC * (G * m + i) + NC] = U[i] * (Z[0][i] > 0)
    return {"y": y}

from concourse.bass import DstId, RemoteDMATransfer
from concourse.mybir import dt, AluOpType, ActivationFunctionType

NCOL = 128
H = 64
WORLD = 512
CF = 0.041
X4 = "float8_e4m3fn_x4"

SCRATCH = {
    "xin": ("sbuf", [128, 512], "bfloat16"),
    "win": ("sbuf", [128, 1024], "bfloat16"),
    "vin": ("sbuf", [128, 1024], "bfloat16"),
    "wq": ("sbuf", [128, 256], X4), "ws": ("sbuf", [128, 256], "uint8"),
    "vq": ("sbuf", [128, 256], X4), "vs": ("sbuf", [128, 256], "uint8"),
    "aq": ("sbuf", [128, 128], X4), "as_": ("sbuf", [128, 128], "uint8"),
    "bq": ("sbuf", [128, 128], X4), "bs": ("sbuf", [128, 128], "uint8"),
    "eq": ("sbuf", [128, 128], X4), "es": ("sbuf", [128, 128], "uint8"),
    "tq": ("sbuf", [128, 128], X4), "ts": ("sbuf", [128, 128], "uint8"),
    "uq": ("sbuf", [128, 128], X4), "us": ("sbuf", [128, 128], "uint8"),
    "ta": ("sbuf", [128, 512], "bfloat16"), "tb": ("sbuf", [128, 512], "bfloat16"),
    "m0": ("sbuf", [128, 128], "float32"), "m1": ("sbuf", [128, 128], "float32"),
    "m2": ("sbuf", [128, 128], "float32"), "m3": ("sbuf", [128, 128], "float32"),
    "yo": ("sbuf", [128, 256], "float32"),
    "z": ("psum", [128, 1024], "float32"), "u": ("psum", [128, 1024], "float32"),
}
SEMAPHORES = ["ld_x", "ld_w", "ld_v", "q_x", "q_w", "q_v", "a_in", "b_in", "e_in", "z0", "z1", "ta_done", "q_a",
              "msk", "u0", "u1", "tb_done", "q_b", "y0", "y1", "st", "sent"]

PLAN = {}


def _bits(m):
    return [1 << k for k in range(m.bit_length()) if m >> k & 1]


def _part(m, k, n):
    b = _bits(m)
    w = len(b) // n
    return sum(b[k * w:k * w + w])


def _plan(T, topo):
    if PLAN:
        return PLAN
    R = list(T.cores)
    n = len(R)
    code, plane = [], []
    for s in range(n):
        t = R[s + 1] if s + 1 < n else R[s - 1]
        own = [c for c in range(WORLD) if c != R[s] and topo.host(c) == topo.host(R[s])
               and topo.chip(c) == topo.chip(R[s]) and topo.may_write(c, t)]
        code.append([c for c in own if topo.die(c) == topo.die(R[s])][0])
        plane.append([c for c in own if topo.die(c) != topo.die(R[s])][0])
    even = [d for d in range(WORLD) if topo.chip(d) == topo.chip(R[0])]
    xr = [c for c in range(WORLD) if topo.same_plane(R[-1], c) and topo.may_write(R[-1], c) and topo.may_write(c, R[0])
          and any(topo.mates(c, d) for d in even)]
    PLAN.update(R=R, n=n, code=code, plane=plane,
                xcode=[c for c in xr if topo.die(c) == topo.die(R[-1])][0],
                xplane=[c for c in xr if topo.die(c) != topo.die(R[-1])][0])
    return PLAN


def rank_program(g, core, T, topo):
    P = _plan(T, topo)
    R, n, code, plane = P["R"], P["n"], P["code"], P["plane"]
    last = n - 1
    S = T.sem
    sent = [0]

    def cut(name, lo, hi):
        v = T[name][:, lo:hi]
        return v.bitcast(dt.uint8) if name.endswith("q") else v

    def send(dst, sem, dname, sname, lo=0, hi=NCOL, mask=None):
        rid, pid = topo.addr(dst, core)
        m = topo.mask(core, dst) if mask is None else mask
        g.remote_dma(cut(dname, lo, hi), cut(sname, lo, hi), S[sem], S["sent"], pid, rid, m)
        sent[0] += len(_bits(m))

    def send_two(parts, sem, name):
        tr = []
        for k, (dst, lo, hi) in enumerate(parts):
            rid, pid = topo.addr(dst, core)
            m = _part(topo.mask(core, dst), k, len(parts))
            tr.append(RemoteDMATransfer(dst_ids=[DstId(rid=rid, pnc=pid)], dma_engine_mask=m, remote_sem=S[sem],
                                        src=cut(name, lo, hi), dst=cut(name, lo, hi)))
            sent[0] += len(_bits(m))
        g.remote_dma_fused(tr, local_sem=S["sent"])

    def finish():
        if sent[0]:
            g.wait_ge(S["sent"], sent[0])

    def count(src, dst):
        return len(_bits(topo.mask(src, dst)))

    back_mask = {s: topo.mask(R[s], code[s]) for s in range(n)}
    back_mask[last] = topo.mask(R[last], P["xcode"])

    if core == P["xcode"] or core == P["xplane"]:
        nm = "aq" if core == P["xcode"] else "as_"
        g.wait_ge(S["a_in"], count(R[last], core))
        send(R[0], "a_in", nm, nm)
        finish()
        return
    if core in code:
        s = code.index(core)
        if s == 0:
            g.wait_ge(S["e_in"], count(R[0], core))
            send_two([(R[1], 0, 32), (R[3], 32, 64)], "e_in", "eq")
        elif s == 1:
            g.wait_ge(S["e_in"], count(R[1], core))
            send(code[3], "e_in", "eq", "eq", 0, 32)
        elif s == 2:
            g.wait_ge(S["e_in"], count(R[2], core))
            send(R[4], "e_in", "eq", "eq", H, NCOL)
        elif s == 3:
            g.wait_ge(S["e_in"], count(code[1], core) + count(R[3], core))
            send(code[5], "e_in", "eq", "eq", 0, H)
        elif s == 4:
            g.wait_ge(S["e_in"], count(R[4], core))
            send(R[5], "e_in", "eq", "eq", H, NCOL)
        else:
            g.wait_ge(S["e_in"], count(code[3], core))
            send(R[5], "e_in", "eq", "eq", 0, H, mask=topo.mask(core, R[4]))
    elif core in plane:
        s = plane.index(core)
        if s == 0:
            g.wait_ge(S["e_in"], count(R[0], core))
            send_two([(plane[1], 0, H), (plane[2], H, NCOL)], "e_in", "es")
        elif s == 1:
            g.wait_ge(S["e_in"], count(plane[0], core) // 2)
            send(plane[3], "e_in", "es", "es", 0, H)
        elif s == 2:
            g.wait_ge(S["e_in"], count(plane[0], core) // 2)
            send(plane[4], "e_in", "es", "es", H, NCOL)
        elif s == 3:
            g.wait_ge(S["e_in"], count(plane[1], core))
            send(plane[5], "e_in", "es", "es", 0, H)
        elif s == 4:
            g.wait_ge(S["e_in"], count(plane[2], core))
            send(R[5], "e_in", "es", "es", H, NCOL)
        else:
            g.wait_ge(S["e_in"], count(plane[3], core))
            send(R[5], "e_in", "es", "es", 0, H, mask=topo.mask(core, R[4]))
    if core in code or core in plane:
        an, bn = ("aq", "bq") if core in code else ("as_", "bs")
        if s < last:
            g.wait_ge(S["a_in"], count(R[s], core))
            send(R[s + 1], "a_in", an, an)
        if s > 0:
            g.wait_ge(S["b_in"], len(_bits(back_mask[s])))
            send(R[s - 1], "b_in", bn, bn)
        finish()
        return

    s = T.rank_of(core)
    if s is None:
        return

    if s in (0, last):
        g.sync.dma_start(T.xin[:], (T.e if s == 0 else T.x)[:]).then_inc(S["ld_x"], 16)
        g.scalar.wait_ge(S["ld_x"], 16)
        g.sync.wait_ge(S["ld_x"], 16)
    g.scalar.dma_start(T.win[:], T.w[:]).then_inc(S["ld_w"], 16)
    g.sync.dma_start(T.vin[:], T.v[:]).then_inc(S["ld_v"], 16)
    V = g.vector
    if s in (0, last):
        V.wait_ge(S["ld_x"], 16)
        qn, sn = ("eq", "es") if s == 0 else ("tq", "ts")
        V.quantize_mx(T[qn][:], T[sn][:], T.xin[:]).then_inc(S["q_x"], 1)
    V.wait_ge(S["ld_w"], 16)
    V.quantize_mx(T.wq[:], T.ws[:], T.win[:]).then_inc(S["q_w"], 1)
    V.wait_ge(S["ld_v"], 16)
    V.quantize_mx(T.vq[:], T.vs[:], T.vin[:]).then_inc(S["q_v"], 1)

    z = [T.z[:, 0:NCOL], T.z[:, 512:512 + NCOL]]
    u = [T.u[:, 0:NCOL], T.u[:, 512:512 + NCOL]]
    m = [T.m0, T.m1, T.m2, T.m3]
    A = AluOpType

    came_a = count(P["xcode"], R[0]) + count(P["xplane"], R[0]) if s == 0 else \
        count(code[s - 1], core) + count(plane[s - 1], core)
    te = g.tensor
    te.wait_ge(S["q_w"], 1)
    te.wait_ge(S["a_in"], came_a)
    for i in range(2):
        c = slice(NCOL * i, NCOL * i + NCOL)
        te.matmul_mx(z[i], T.wq[:, c], T.ws[:, c], T.aq[:], T.as_[:], True, True).then_inc(S["z%d" % i], 1)
    te.wait_ge(S["q_v"], 1)
    if s == last:
        te.wait_ge(S["e_in"], count(code[5], R[4]) + count(code[4], core) + count(plane[5], R[4]) + count(plane[4], core))
        bq, bs = T.eq, T.es
    else:
        te.wait_ge(S["b_in"], count(code[s + 1], core) + count(plane[s + 1], core))
        bq, bs = T.bq, T.bs
    for i in range(2):
        c = slice(NCOL * i, NCOL * i + NCOL)
        te.matmul_mx(u[i], T.vq[:, c], T.vs[:, c], bq[:], bs[:], True, True).then_inc(S["u%d" % i], 1)

    if s < last:
        relu = ActivationFunctionType.Relu
        g.scalar.wait_ge(S["z0"], 1)
        for b, f in ((0, CF), (1, -CF)):
            g.scalar.activation(T.ta[:, b:512:4], z[0], relu, scale=f).then_inc(S["ta_done"], 1)
        V.wait_ge(S["z1"], 1)
        for b, f in ((2, CF), (3, -CF)):
            V.tensor_scalar(T.ta[:, b:512:4], z[1], f, 0.0, A.mult, A.max).then_inc(S["ta_done"], 1)
        V.wait_ge(S["ta_done"], 4)
        V.quantize_mx(T.tq[:], T.ts[:], T.ta[:]).then_inc(S["q_a"], 1)
    if s == 0:
        need = ((0, 0, A.is_gt, 1.0), (2, 1, A.is_gt, 1.0))
    else:
        need = ((0, 0, A.is_gt, CF), (1, 0, A.is_lt, -CF), (2, 1, A.is_gt, CF), (3, 1, A.is_lt, -CF))
    for k, i, op, f in need:
        V.wait_ge(S["z%d" % i], 1)
        V.tensor_scalar(m[k][:], z[i], 0.0, f, op, A.mult).then_inc(S["msk"], 1)
    V.wait_ge(S["msk"], len(need))

    if s == 0:
        for i, q in ((0, g.sync), (1, g.scalar)):
            c = slice(NCOL * i, NCOL * i + NCOL)
            V.wait_ge(S["u%d" % i], 1)
            V.tensor_tensor(T.yo[:, c], u[i], m[2 * i][:], A.mult).then_inc(S["y%d" % i], 1)
            q.wait_ge(S["y%d" % i], 1)
            q.dma_start(T.y[:, c], T.yo[:, c]).then_inc(S["st"], 16)
        g.sync.wait_ge(S["st"], 32)
    else:
        for b in range(4):
            V.wait_ge(S["u%d" % (b // 2)], 1)
            V.tensor_tensor(T.tb[:, b:512:4], u[b // 2], m[b][:], A.mult).then_inc(S["tb_done"], 1)
        V.wait_ge(S["tb_done"], 4)
        V.quantize_mx(T.uq[:], T.us[:], T.tb[:]).then_inc(S["q_b"], 1)

    if s == last:
        g.wait_ge(S["q_x"], 1)
        send(P["xcode"], "a_in", "aq", "tq")
        send(P["xplane"], "a_in", "as_", "ts")
    elif s == 0:
        g.wait_ge(S["q_x"], 1)
        send(code[0], "e_in", "eq", "eq", 0, H)
        send(plane[0], "e_in", "es", "es")
        send(R[2], "e_in", "eq", "eq", H, NCOL)
    elif s in (1, 2, 3, 4):
        lo, hi = {1: (0, 32), 2: (H, NCOL), 3: (32, H), 4: (H, NCOL)}[s]
        frm = {1: code[0], 2: R[0], 3: code[0], 4: code[2]}[s]
        g.wait_ge(S["e_in"], count(frm, core) // (2 if frm == code[0] else 1))
        send(code[s], "e_in", "eq", "eq", lo, hi)
    if s < last:
        g.wait_ge(S["q_a"], 1)
        send(code[s], "a_in", "aq", "tq")
        send(plane[s], "a_in", "as_", "ts")
    if s > 0:
        g.wait_ge(S["q_b"], 1)
        send(code[s], "b_in", "bq", "uq", mask=back_mask[s])
        send(plane[s], "b_in", "bs", "us", mask=back_mask[s])
    finish()
